import numpy as np
import ml_dtypes


def mxq(x, axis, fmt="e4m3"):
    dtype, down = {"e4m3": (ml_dtypes.float8_e4m3fn, 7), "e5m2": (ml_dtypes.float8_e5m2, 14)}[fmt]
    v = np.moveaxis(np.asarray(x, np.float32).astype(ml_dtypes.bfloat16).astype(np.float64), axis, -1)
    blocks = v.reshape(v.shape[:-1] + (-1, 32))
    amax = np.abs(blocks).max(-1, keepdims=True)
    byte = np.maximum(np.where(amax > 0, np.frexp(amax)[1] - 1 + 127, 0) - down, 1)
    scale = np.exp2(byte - 127.0)
    codes = (blocks / scale).astype(np.float32).astype(dtype).astype(np.float64)
    return np.moveaxis((codes * scale).reshape(v.shape), -1, axis)


WIDE = False


def mx_kscale(k):
    if not WIDE:
        return np.ones(k)
    levels = np.array([10, -10, 5, -5, 0])
    if k % 512:
        return np.exp2(np.random.permutation(np.resize(levels, k // 32))).repeat(32)
    a = np.empty((k // 512, 16))
    for p in range(k // 512):
        a[p, :8] = np.random.permutation(np.resize(levels, 8))
        for g in range(8):
            far = levels[np.abs(levels - a[p, g]) >= 10]
            a[p, g + 8] = far[np.random.randint(len(far))]
    return np.exp2(a.ravel()).repeat(32)


def f64(x):
    return np.asarray(x).astype(np.float64)


def striped(idx):
    return np.tile(idx.reshape(-1, 16).T, (8, 1)).astype(np.uint16)


def unstriped(offs):
    return offs[:16].T.reshape(-1).astype(np.int64)


E2M1 = np.array([0.0, 0.5, 1.0, 1.5, 2.0, 3.0, 4.0, 6.0, -0.0, -0.5, -1.0, -1.5, -2.0, -3.0, -4.0, -6.0])


def pack_weight(w, fmt):
    k, n = w.shape
    w = f64(np.asarray(w, np.float32).astype(ml_dtypes.bfloat16)).reshape(k // 32, 32, n)
    amax = np.abs(w).max(1)
    if fmt == "e4m3":
        byte = np.frexp(amax)[1] - 1 + 127 - 7
    else:
        mant, ex = np.frexp(amax / 6.0)
        byte = np.where(mant > 0.5, ex, ex - 1) + 127
    byte = np.clip(np.where(amax > 0, byte, 1), 1, 254)
    scaled = (w * np.exp2(127.0 - byte)[:, None, :]).reshape(k, n).astype(np.float32)
    by_word = np.ascontiguousarray(scaled.reshape(k // 512, 128, 4, n).transpose(0, 1, 3, 2))
    if fmt == "e4m3":
        words = by_word.astype(ml_dtypes.float8_e4m3fn).view(np.uint8)
    else:
        c = by_word.astype(ml_dtypes.float4_e2m1fn).view(np.uint8) & 0xF
        words = (c[..., 0::2] | (c[..., 1::2] << 4)).reshape(k // 512, 128, 2 * n)
    return np.ascontiguousarray(words), np.ascontiguousarray(byte.astype(np.uint8).reshape(k // 512, 16, n))


def unpack_weight(words, scales, fmt):
    g, _, n = scales.shape
    words = np.ascontiguousarray(words).reshape(g, 128, n, -1)
    if fmt == "e4m3":
        vals = words.view(ml_dtypes.float8_e4m3fn).astype(np.float64)
    else:
        nib = np.empty((g, 128, n, 4), np.uint8)
        nib[..., 0::2] = words & 0xF
        nib[..., 1::2] = words >> 4
        vals = E2M1[nib]
    vals = vals * np.repeat(np.exp2(scales.astype(np.float64) - 127.0), 8, axis=1)[..., None]
    return vals.transpose(0, 1, 3, 2).reshape(g * 512, n)


def silu(v):
    return v / (1.0 + np.exp(-np.maximum(v, -700.0)))


K, T, E, N = 2560, 512, 4, 128
COUNTS = (128, 384, 256, 256)
STARTS = np.cumsum((0,) + COUNTS)


def by_expert(wq, xq):
    return np.concatenate([wq[e].T @ xq[:, STARTS[e]:STARTS[e + 1]] for e in range(E)], axis=1)


def setup_inputs():
    n = np.random.standard_normal
    s = mx_kscale(K)[:, None]
    both = np.repeat(np.arange(E), COUNTS)
    pair = np.stack([both[:T], both[T:]])[:, np.random.permutation(T)]
    pair = np.where(np.random.rand(T) < 0.5, pair, pair[::-1])
    order = np.argsort(pair.reshape(-1), kind="stable")
    slot_token = order % T; pos = np.empty(2 * T, np.int64); pos[order] = np.arange(2 * T); pos = pos.reshape(2, T)
    g = np.random.uniform(0.2, 0.8, T)
    w = [pack_weight(m, "e2m1") for m in n((E, K, N)) / np.sqrt(K) / s[None]]
    return {
        "xT": (n((K, T)) * s).astype(np.float32),
        "w_words": np.stack([m[0] for m in w]),
        "w_scales": np.stack([m[1] for m in w]),
        "b": (0.3 * n((N, E))).astype(np.float32),
        "gate": np.stack([np.tile(g, (N, 1)), np.tile(1.0 - g, (N, 1))]).astype(np.float32),
        "offs": striped(slot_token),
        "pos1": striped(pos[0]),
        "pos2": striped(pos[1]),
    }


def reference(xT, w_words, w_scales, b, gate, offs, pos1, pos2):
    idx = unstriped(offs)
    w = np.stack([unpack_weight(w_words[e], w_scales[e], "e2m1") for e in range(E)])
    xq = mxq(f64(xT)[:, idx], 0, "e4m3")
    y = by_expert(w, xq)
    y = silu(y + np.repeat(f64(b), COUNTS, axis=1))
    return f64(gate[0]) * y[:, unstriped(pos1)] + f64(gate[1]) * y[:, unstriped(pos2)]

@@ -1,0 +1,169 @@
+from contextlib import ExitStack
+
+import concourse.mybir as mybir
+
+K, T, N = 2560, 512, 128
+COUNTS = (128, 384, 256, 256)
+E = len(COUNTS)
+SLOTS = sum(COUNTS)
+
+FLOPS = 2 * K * N * SLOTS
+
+F32 = mybir.dt.float32
+BF16 = mybir.dt.bfloat16
+U32 = mybir.dt.uint32
+I32 = mybir.dt.int32
+U16 = mybir.dt.uint16
+U8 = mybir.dt.uint8
+FP8X4 = mybir.dt.float8_e4m3fn_x4
+FP4X4 = mybir.dt.float4_e2m1fn_x4
+SILU = mybir.ActivationFunctionType.Silu
+MULT = mybir.AluOpType.mult
+ADD = mybir.AluOpType.add
+
+P = 128
+PACK = 4
+K_PASS = P * PACK
+PASSES = K // K_PASS
+BLOCK = 128
+BLOCKS = SLOTS // BLOCK
+BLOCK_EXPERT = [e for e in range(E) for i in range(COUNTS[e] // BLOCK)]
+WINDOW = 1536
+LAST_CODE_PIECES = ((0, 384), (384, 768), (768, 1024))
+
+
+def tile_moe_rag_lin_silu_kernel(tc, xT, w_words, w_scales, b, gate, offs, pos1, pos2, out):
+    nc = tc.nc
+    with ExitStack() as ctx:
+        keep = ctx.enter_context(tc.tile_pool(name="keep", bufs=1))
+        psum = ctx.enter_context(tc.psum_pool(name="psum", bufs=1))
+
+        offs_sb = keep.tile([P, SLOTS // 16], U16)
+        pos1_sb = keep.tile([P, T // 16], U16)
+        pos2_sb = keep.tile([P, T // 16], U16)
+
+        raw = [keep.tile([P, PACK, T], F32, name=f"raw{a}") for a in range(PASSES)]
+        grouped = [keep.tile([P, T * PACK], BF16, name=f"grouped{a}", align_bytes=64) for a in range(PASSES)]
+        codes = keep.tile([P, (PASSES - 1) * T + WINDOW], I32, align_bytes=64)
+        scales = keep.tile([P, T + WINDOW], U8, align_bytes=64)
+        slot_codes = [keep.tile([P, SLOTS], U32, name=f"slot_codes{a}", align_bytes=64) for a in range(PASSES)]
+        slot_packed = keep.tile([P, SLOTS], U8, align_bytes=64)
+        slot_last = keep.tile([P, SLOTS], U8, align_bytes=64)
+        moved = [keep.tile([P, SLOTS], U8, name=f"moved{a}", align_bytes=64) for a in range(1, 4)]
+        slot_scales = [slot_packed] + moved + [slot_last]
+        w_sb = keep.tile([P, E * PASSES, 2 * N], U8, align_bytes=64)
+        ws_sb = keep.tile([P, E * PASSES, N], U8, align_bytes=64)
+        b_sb = keep.tile([P, E], F32)
+        gate_sb = [keep.tile([P, T], F32, name=f"gate{i}") for i in range(2)]
+        y = keep.tile([P, SLOTS], F32)
+        part1 = keep.tile([P, T], F32)
+        part2 = keep.tile([P, T], F32)
+        result = keep.tile([P, T], F32)
+        dummy = keep.tile([P, 8], F32)
+        banks = [psum.tile([P, BLOCK], F32, name=f"bank{i}") for i in range(BLOCKS)]
+
+        nc.vector.memset(dummy[:, 0:1], 0.0)
+        nc.scalar.activation(dummy[:, 4:5], dummy[:, 0:1], SILU)
+
+        nc.vector.memset(codes[:, PASSES * T :], 0)
+        nc.gpsimd.memset(scales[:].bitcast(I32), 0)
+        for tile in moved:
+            nc.gpsimd.memset(tile[:].bitcast(I32), 0)
+        nc.gpsimd.memset(ws_sb[:].rearrange("p i n -> p (i n)").bitcast(I32), 0)
+
+        def x_rows(a):
+            return xT[a * K_PASS : (a + 1) * K_PASS, :].rearrange("(p j) t -> p j t", j=PACK)
+
+        half = T // 2
+        for a in range(2):
+            for t0 in (0, half):
+                nc.sync.dma_start(raw[a][:, :, t0 : t0 + half], x_rows(a)[:, :, t0 : t0 + half])
+            if a == 0:
+                nc.sync.dma_start(offs_sb[:], offs)
+        for a in range(2, PASSES):
+            nc.sync.dma_start(raw[a][:], x_rows(a))
+        ws_words = w_scales.bitcast(I32).rearrange("e a q n -> q (e a) n")
+        for q in range(4):
+            nc.sync.dma_start(ws_sb[32 * q : 32 * q + 4].bitcast(I32), ws_words[4 * q : 4 * q + 4])
+        nc.sync.dma_start(w_sb[:].bitcast(I32), w_words.bitcast(I32).rearrange("e a p n -> p (e a) n"))
+        nc.sync.dma_start(b_sb[:], b)
+        nc.sync.dma_start(pos1_sb[:], pos1)
+        nc.sync.dma_start(pos2_sb[:], pos2)
+        for i in range(2):
+            nc.sync.dma_start(gate_sb[i][:], gate[i])
+
+        def interleave(copy, a, t0, t1):
+            dst = grouped[a][:, PACK * t0 : PACK * t1].rearrange("p (c i j) -> p c j i", i=4, j=PACK)
+            copy(dst, raw[a][:, :, t0:t1].rearrange("p j (c i) -> p c j i", i=4))
+
+        def quantize(a, t0, t1):
+            nc.vector.quantize_mx(
+                out=codes[:, T * (PASSES - 1 - a) + t0 : T * (PASSES - 1 - a) + t1].bitcast(FP8X4),
+                scales=scales[4 * a : P, T + t0 : T + t1] if a < 4 else scales[:, t0:t1],
+                in_=grouped[a][:, PACK * t0 : PACK * t1],
+            )
+
+        def gather(dst, window, s0, s1):
+            nc.vector.tensor_copy(dst[:, s0:s1], window.indirect(offs_sb[:, s0 // 16 : s1 // 16]))
+
+        def multiply(a, i):
+            e = BLOCK_EXPERT[i]
+            cols = slice(i * BLOCK, (i + 1) * BLOCK)
+            nc.tensor.matmul_mx(
+                out=banks[i][:],
+                lhsT=w_sb[:, e * PASSES + a, :].bitcast(FP4X4),
+                lhsT_scale=ws_sb[:, e * PASSES + a, :],
+                rhs=slot_codes[a][:, cols].bitcast(FP8X4),
+                rhs_scale=slot_scales[a][:, cols],
+                start=(a == 0),
+                stop=(a == PASSES - 1),
+            )
+
+        def gather_codes(a, s0, s1):
+            first = T * (PASSES - 1 - a)
+            gather(slot_codes[a], codes[:, first : first + WINDOW].bitcast(U32), s0, s1)
+
+        for t0 in (0, half):
+            interleave(nc.vector.tensor_copy, 0, t0, t0 + 176)
+            interleave(nc.scalar.copy, 0, t0 + 176, t0 + half)
+            quantize(0, t0, t0 + half)
+        interleave(nc.scalar.copy, 1, 0, half)
+        interleave(nc.scalar.copy, 1, half, 384)
+        for a in range(2, PASSES):
+            interleave(nc.scalar.copy, a, 0, half)
+            interleave(nc.scalar.copy, a, half, T)
+        gather_codes(0, 0, SLOTS)
+        interleave(nc.vector.tensor_copy, 1, 384, T)
+        quantize(1, 0, T)
+        gather_codes(1, 0, SLOTS)
+        quantize(2, 0, T)
+        gather_codes(2, 0, SLOTS)
+        quantize(3, 0, T)
+        gather(slot_packed, scales[:, T : T + WINDOW], 0, SLOTS)
+        for a in range(1, 4):
+            for r in range(4):
+                nc.sync.dma_start(moved[a - 1][r:P:32].bitcast(I32), slot_packed[4 * a + r : P : 32].bitcast(I32))
+        quantize(4, 0, T)
+        for i in range(BLOCKS):
+            multiply(0, i)
+        gather_codes(3, 0, SLOTS)
+        for a in (1, 2, 3):
+            for i in range(BLOCKS):
+                multiply(a, i)
+        gather(slot_last, scales[:, 0:WINDOW], 0, SLOTS)
+        for s0, s1 in LAST_CODE_PIECES:
+            gather_codes(4, s0, s1)
+            for i in range(s0 // BLOCK, s1 // BLOCK):
+                multiply(4, i)
+        for i in range(BLOCKS):
+            e = BLOCK_EXPERT[i]
+            nc.scalar.activation(y[:, i * BLOCK : (i + 1) * BLOCK], banks[i][:], SILU, bias=b_sb[:, e : e + 1])
+
+        nc.vector.tensor_tensor(part1[:], y[:].indirect(pos1_sb[:]), gate_sb[0][:], MULT)
+        halves = (slice(0, half), slice(half, T))
+        for h in range(2):
+            listed = pos2_sb[:, h * (half // 16) : (h + 1) * (half // 16)]
+            nc.vector.tensor_tensor(part2[:, halves[h]], y[:].indirect(listed), gate_sb[1][:, halves[h]], MULT)
+        for h in range(2):
+            nc.vector.tensor_tensor(result[:, halves[h]], part1[:, halves[h]], part2[:, halves[h]], ADD)
+            nc.sync.dma_start(out[:, halves[h]], result[:, halves[h]])

@@ -28,8 +28,9 @@ PASSES = K // K_PASS
 BLOCK = 128
 BLOCKS = SLOTS // BLOCK
 BLOCK_EXPERT = [e for e in range(E) for i in range(COUNTS[e] // BLOCK)]
+V_FROM = 384
 WINDOW = 1536
-LAST_CODE_PIECES = ((0, 384), (384, 768), (768, 1024))
+LAST_CODE_PIECES = ((0, 512), (512, 896), (896, 1024))
 
 
 def tile_moe_rag_lin_silu_kernel(tc, xT, w_words, w_scales, b, gate, offs, pos1, pos2, out):
@@ -121,28 +122,31 @@ def tile_moe_rag_lin_silu_kernel(tc, xT, w_words, w_scales, b, gate, offs, pos1,
 
         def gather_codes(a, s0, s1):
             first = T * (PASSES - 1 - a)
-            gather(slot_codes[a], codes[:, first : first + WINDOW].bitcast(U32), s0, s1)
+            window = WINDOW if s1 - s0 > 128 else 2 * T
+            gather(slot_codes[a], codes[:, first : first + window].bitcast(U32), s0, s1)
 
         for t0 in (0, half):
             interleave(nc.vector.tensor_copy, 0, t0, t0 + 176)
             interleave(nc.scalar.copy, 0, t0 + 176, t0 + half)
             quantize(0, t0, t0 + half)
         interleave(nc.scalar.copy, 1, 0, half)
-        interleave(nc.scalar.copy, 1, half, 384)
+        interleave(nc.scalar.copy, 1, half, 336)
         for a in range(2, PASSES):
-            interleave(nc.scalar.copy, a, 0, half)
-            interleave(nc.scalar.copy, a, half, T)
+            interleave(nc.scalar.copy, a, 0, V_FROM)
         gather_codes(0, 0, SLOTS)
-        interleave(nc.vector.tensor_copy, 1, 384, T)
+        interleave(nc.vector.tensor_copy, 1, 336, T)
         quantize(1, 0, T)
         gather_codes(1, 0, SLOTS)
+        interleave(nc.vector.tensor_copy, 2, V_FROM, T)
         quantize(2, 0, T)
         gather_codes(2, 0, SLOTS)
+        interleave(nc.vector.tensor_copy, 3, V_FROM, T)
         quantize(3, 0, T)
         gather(slot_packed, scales[:, T : T + WINDOW], 0, SLOTS)
         for a in range(1, 4):
             for r in range(4):
                 nc.sync.dma_start(moved[a - 1][r:P:32].bitcast(I32), slot_packed[4 * a + r : P : 32].bitcast(I32))
+        interleave(nc.vector.tensor_copy, 4, V_FROM, T)
         quantize(4, 0, T)
         for i in range(BLOCKS):
             multiply(0, i)
@@ -160,10 +164,10 @@ def tile_moe_rag_lin_silu_kernel(tc, xT, w_words, w_scales, b, gate, offs, pos1,
             nc.scalar.activation(y[:, i * BLOCK : (i + 1) * BLOCK], banks[i][:], SILU, bias=b_sb[:, e : e + 1])
 
         nc.vector.tensor_tensor(part1[:], y[:].indirect(pos1_sb[:]), gate_sb[0][:], MULT)
-        halves = (slice(0, half), slice(half, T))
-        for h in range(2):
-            listed = pos2_sb[:, h * (half // 16) : (h + 1) * (half // 16)]
-            nc.vector.tensor_tensor(part2[:, halves[h]], y[:].indirect(listed), gate_sb[1][:, halves[h]], MULT)
-        for h in range(2):
-            nc.vector.tensor_tensor(result[:, halves[h]], part1[:, halves[h]], part2[:, halves[h]], ADD)
-            nc.sync.dma_start(out[:, halves[h]], result[:, halves[h]])
+        parts = (slice(0, 384), slice(384, T))
+        for cols in parts:
+            listed = pos2_sb[:, cols.start // 16 : cols.stop // 16]
+            nc.vector.tensor_tensor(part2[:, cols], y[:].indirect(listed), gate_sb[1][:, cols], MULT)
+        for cols in parts:
+            nc.vector.tensor_tensor(result[:, cols], part1[:, cols], part2[:, cols], ADD)
+            nc.sync.dma_start(out[:, cols], result[:, cols])

@@ -28,7 +28,6 @@ PASSES = K // K_PASS
 BLOCK = 128
 BLOCKS = SLOTS // BLOCK
 BLOCK_EXPERT = [e for e in range(E) for i in range(COUNTS[e] // BLOCK)]
-V_FROM = 384
 WINDOW = 1536
 LAST_CODE_PIECES = ((0, 512), (512, 896), (896, 1024))
 
@@ -72,10 +71,11 @@ def tile_moe_rag_lin_silu_kernel(tc, xT, w_words, w_scales, b, gate, offs, pos1,
             nc.gpsimd.memset(tile[:].bitcast(I32), 0)
         nc.gpsimd.memset(ws_sb[:].rearrange("p i n -> p (i n)").bitcast(I32), 0)
 
+        half = T // 2
+
         def x_rows(a):
             return xT[a * K_PASS : (a + 1) * K_PASS, :].rearrange("(p j) t -> p j t", j=PACK)
 
-        half = T // 2
         for a in range(2):
             for t0 in (0, half):
                 nc.sync.dma_start(raw[a][:, :, t0 : t0 + half], x_rows(a)[:, :, t0 : t0 + half])
@@ -88,10 +88,6 @@ def tile_moe_rag_lin_silu_kernel(tc, xT, w_words, w_scales, b, gate, offs, pos1,
             nc.sync.dma_start(ws_sb[32 * q : 32 * q + 4].bitcast(I32), ws_words[4 * q : 4 * q + 4])
         nc.sync.dma_start(w_sb[:].bitcast(I32), w_words.bitcast(I32).rearrange("e a p n -> p (e a) n"))
         nc.sync.dma_start(b_sb[:], b)
-        nc.sync.dma_start(pos1_sb[:], pos1)
-        nc.sync.dma_start(pos2_sb[:], pos2)
-        for i in range(2):
-            nc.sync.dma_start(gate_sb[i][:], gate[i])
 
         def interleave(copy, a, t0, t1):
             dst = grouped[a][:, PACK * t0 : PACK * t1].rearrange("p (c i j) -> p c j i", i=4, j=PACK)
@@ -126,27 +122,30 @@ def tile_moe_rag_lin_silu_kernel(tc, xT, w_words, w_scales, b, gate, offs, pos1,
             gather(slot_codes[a], codes[:, first : first + window].bitcast(U32), s0, s1)
 
         for t0 in (0, half):
-            interleave(nc.vector.tensor_copy, 0, t0, t0 + 176)
-            interleave(nc.scalar.copy, 0, t0 + 176, t0 + half)
+            interleave(nc.vector.tensor_copy, 0, t0, t0 + 144)
+            interleave(nc.scalar.copy, 0, t0 + 144, t0 + half)
             quantize(0, t0, t0 + half)
-        interleave(nc.scalar.copy, 1, 0, half)
-        interleave(nc.scalar.copy, 1, half, 336)
+        interleave(nc.vector.tensor_copy, 1, 0, 128)
+        interleave(nc.scalar.copy, 1, 128, half)
+        interleave(nc.scalar.copy, 1, half, T)
         for a in range(2, PASSES):
-            interleave(nc.scalar.copy, a, 0, V_FROM)
+            interleave(nc.scalar.copy, a, 0, T)
         gather_codes(0, 0, SLOTS)
-        interleave(nc.vector.tensor_copy, 1, 336, T)
         quantize(1, 0, T)
-        gather_codes(1, 0, SLOTS)
-        interleave(nc.vector.tensor_copy, 2, V_FROM, T)
+        gather_codes(1, 0, 512)
         quantize(2, 0, T)
-        gather_codes(2, 0, SLOTS)
-        interleave(nc.vector.tensor_copy, 3, V_FROM, T)
+        gather_codes(1, 512, SLOTS)
+        gather_codes(2, 0, 512)
         quantize(3, 0, T)
+        gather_codes(2, 512, SLOTS)
         gather(slot_packed, scales[:, T : T + WINDOW], 0, SLOTS)
         for a in range(1, 4):
             for r in range(4):
                 nc.sync.dma_start(moved[a - 1][r:P:32].bitcast(I32), slot_packed[4 * a + r : P : 32].bitcast(I32))
-        interleave(nc.vector.tensor_copy, 4, V_FROM, T)
+        nc.sync.dma_start(pos1_sb[:], pos1)
+        nc.sync.dma_start(pos2_sb[:], pos2)
+        for i in range(2):
+            nc.sync.dma_start(gate_sb[i][:], gate[i])
         quantize(4, 0, T)
         for i in range(BLOCKS):
             multiply(0, i)

@@ -25,11 +25,12 @@ P = 128
 PACK = 4
 K_PASS = P * PACK
 PASSES = K // K_PASS
+SHARED = 4
 BLOCK = 128
 BLOCKS = SLOTS // BLOCK
 BLOCK_EXPERT = [e for e in range(E) for i in range(COUNTS[e] // BLOCK)]
 WINDOW = 1536
-LAST_CODE_PIECES = ((0, 512), (512, 896), (896, 1024))
+HALF = T // 2
 
 
 def tile_moe_rag_lin_silu_kernel(tc, xT, w_words, w_scales, b, gate, offs, pos1, pos2, out):
@@ -41,44 +42,38 @@ def tile_moe_rag_lin_silu_kernel(tc, xT, w_words, w_scales, b, gate, offs, pos1,
         offs_sb = keep.tile([P, SLOTS // 16], U16)
         pos1_sb = keep.tile([P, T // 16], U16)
         pos2_sb = keep.tile([P, T // 16], U16)
-
-        raw = [keep.tile([P, PACK, T], F32, name=f"raw{a}") for a in range(PASSES)]
+        raw = [keep.tile([P, PACK, T], F32, name=f"raw{a}", tag=f"turn{a}", align_bytes=64) for a in range(PASSES)]
         grouped = [keep.tile([P, T * PACK], BF16, name=f"grouped{a}", align_bytes=64) for a in range(PASSES)]
         codes = keep.tile([P, (PASSES - 1) * T + WINDOW], I32, align_bytes=64)
         scales = keep.tile([P, T + WINDOW], U8, align_bytes=64)
         slot_codes = [keep.tile([P, SLOTS], U32, name=f"slot_codes{a}", align_bytes=64) for a in range(PASSES)]
-        slot_packed = keep.tile([P, SLOTS], U8, align_bytes=64)
+        slot_shared = keep.tile([P, SLOTS], U8, align_bytes=64)
         slot_last = keep.tile([P, SLOTS], U8, align_bytes=64)
-        moved = [keep.tile([P, SLOTS], U8, name=f"moved{a}", align_bytes=64) for a in range(1, 4)]
-        slot_scales = [slot_packed] + moved + [slot_last]
-        w_sb = keep.tile([P, E * PASSES, 2 * N], U8, align_bytes=64)
+        moved = [keep.tile([P, SLOTS], U8, name=f"moved{a}", align_bytes=64) for a in range(1, SHARED)]
+        slot_scales = [slot_shared] + moved + [slot_last]
         ws_sb = keep.tile([P, E * PASSES, N], U8, align_bytes=64)
         b_sb = keep.tile([P, E], F32)
-        gate_sb = [keep.tile([P, T], F32, name=f"gate{i}") for i in range(2)]
         y = keep.tile([P, SLOTS], F32)
         part1 = keep.tile([P, T], F32)
         part2 = keep.tile([P, T], F32)
         result = keep.tile([P, T], F32)
-        dummy = keep.tile([P, 8], F32)
+        warm = keep.tile([P, 8], F32)
         banks = [psum.tile([P, BLOCK], F32, name=f"bank{i}") for i in range(BLOCKS)]
 
-        nc.vector.memset(dummy[:, 0:1], 0.0)
-        nc.scalar.activation(dummy[:, 4:5], dummy[:, 0:1], SILU)
-
+        nc.vector.memset(warm[:, 0:1], 0.0)
+        nc.scalar.activation(warm[:, 4:5], warm[:, 0:1], SILU)
         nc.vector.memset(codes[:, PASSES * T :], 0)
         nc.gpsimd.memset(scales[:].bitcast(I32), 0)
-        for tile in moved:
-            nc.gpsimd.memset(tile[:].bitcast(I32), 0)
         nc.gpsimd.memset(ws_sb[:].rearrange("p i n -> p (i n)").bitcast(I32), 0)
-
-        half = T // 2
+        for plane in moved:
+            nc.gpsimd.memset(plane[:].bitcast(I32), 0)
 
         def x_rows(a):
             return xT[a * K_PASS : (a + 1) * K_PASS, :].rearrange("(p j) t -> p j t", j=PACK)
 
         for a in range(2):
-            for t0 in (0, half):
-                nc.sync.dma_start(raw[a][:, :, t0 : t0 + half], x_rows(a)[:, :, t0 : t0 + half])
+            for t0 in (0, HALF):
+                nc.sync.dma_start(raw[a][:, :, t0 : t0 + HALF], x_rows(a)[:, :, t0 : t0 + HALF])
             if a == 0:
                 nc.sync.dma_start(offs_sb[:], offs)
         for a in range(2, PASSES):
@@ -86,7 +81,6 @@ def tile_moe_rag_lin_silu_kernel(tc, xT, w_words, w_scales, b, gate, offs, pos1,
         ws_words = w_scales.bitcast(I32).rearrange("e a q n -> q (e a) n")
         for q in range(4):
             nc.sync.dma_start(ws_sb[32 * q : 32 * q + 4].bitcast(I32), ws_words[4 * q : 4 * q + 4])
-        nc.sync.dma_start(w_sb[:].bitcast(I32), w_words.bitcast(I32).rearrange("e a p n -> p (e a) n"))
         nc.sync.dma_start(b_sb[:], b)
 
         def interleave(copy, a, t0, t1):
@@ -94,14 +88,55 @@ def tile_moe_rag_lin_silu_kernel(tc, xT, w_words, w_scales, b, gate, offs, pos1,
             copy(dst, raw[a][:, :, t0:t1].rearrange("p j (c i) -> p c j i", i=4))
 
         def quantize(a, t0, t1):
+            place = T * (PASSES - 1 - a)
             nc.vector.quantize_mx(
-                out=codes[:, T * (PASSES - 1 - a) + t0 : T * (PASSES - 1 - a) + t1].bitcast(FP8X4),
-                scales=scales[4 * a : P, T + t0 : T + t1] if a < 4 else scales[:, t0:t1],
+                out=codes[:, place + t0 : place + t1].bitcast(FP8X4),
+                scales=scales[4 * a : P, T + t0 : T + t1] if a < SHARED else scales[:, t0:t1],
                 in_=grouped[a][:, PACK * t0 : PACK * t1],
             )
 
         def gather(dst, window, s0, s1):
             nc.vector.tensor_copy(dst[:, s0:s1], window.indirect(offs_sb[:, s0 // 16 : s1 // 16]))
+
+        def gather_codes(a, s0, s1):
+            place = T * (PASSES - 1 - a)
+            width = WINDOW if s1 - s0 > 128 else 2 * T
+            gather(slot_codes[a], codes[:, place : place + width].bitcast(U32), s0, s1)
+
+        for t0 in (0, HALF):
+            interleave(nc.vector.tensor_copy, 0, t0, t0 + 144)
+            interleave(nc.scalar.copy, 0, t0 + 144, t0 + HALF)
+            quantize(0, t0, t0 + HALF)
+        interleave(nc.vector.tensor_copy, 1, 0, 128)
+        interleave(nc.scalar.copy, 1, 128, HALF)
+        interleave(nc.scalar.copy, 1, HALF, T)
+        gather_codes(0, 0, SLOTS)
+        interleave(nc.scalar.copy, 2, 128, T)
+        quantize(1, 0, T)
+        gather_codes(1, 0, 512)
+        interleave(nc.vector.tensor_copy, 2, 0, 128)
+        interleave(nc.scalar.copy, 3, 224, T)
+        gather_codes(1, 512, SLOTS)
+        quantize(2, 0, T)
+        interleave(nc.vector.tensor_copy, 3, 0, 224)
+        w_sb = keep.tile([P, E * PASSES, 2 * N], U8, name="w_sb", tag="turn3", align_bytes=64)
+        nc.scalar.dma_start(w_sb[:].bitcast(I32), w_words.bitcast(I32).rearrange("e a p n -> p (e a) n"))
+        interleave(nc.scalar.copy, 4, 0, T)
+        gather_codes(2, 0, 256)
+        quantize(3, 0, T)
+        gather_codes(2, 256, 512)
+        gather(slot_shared, scales[:, T : T + WINDOW], 0, SLOTS)
+        for a in range(1, SHARED):
+            for r in range(4):
+                nc.sync.dma_start(moved[a - 1][r:P:32].bitcast(I32), slot_shared[4 * a + r : P : 32].bitcast(I32))
+        gather_codes(2, 512, SLOTS)
+        nc.sync.dma_start(pos1_sb[:], pos1)
+        nc.sync.dma_start(pos2_sb[:], pos2)
+        gate_sb = keep.tile([P, 2, T], F32, name="gate_sb", tag="turn4", align_bytes=64)
+        nc.sync.dma_start(gate_sb[:], gate.rearrange("g p t -> p g t"))
+        gather_codes(3, 0, 768)
+        quantize(4, 0, T)
+        gather_codes(3, 768, SLOTS)
 
         def multiply(a, i):
             e = BLOCK_EXPERT[i]
@@ -116,45 +151,11 @@ def tile_moe_rag_lin_silu_kernel(tc, xT, w_words, w_scales, b, gate, offs, pos1,
                 stop=(a == PASSES - 1),
             )
 
-        def gather_codes(a, s0, s1):
-            first = T * (PASSES - 1 - a)
-            window = WINDOW if s1 - s0 > 128 else 2 * T
-            gather(slot_codes[a], codes[:, first : first + window].bitcast(U32), s0, s1)
-
-        for t0 in (0, half):
-            interleave(nc.vector.tensor_copy, 0, t0, t0 + 144)
-            interleave(nc.scalar.copy, 0, t0 + 144, t0 + half)
-            quantize(0, t0, t0 + half)
-        interleave(nc.vector.tensor_copy, 1, 0, 128)
-        interleave(nc.scalar.copy, 1, 128, half)
-        interleave(nc.scalar.copy, 1, half, T)
-        for a in range(2, PASSES):
-            interleave(nc.scalar.copy, a, 0, T)
-        gather_codes(0, 0, SLOTS)
-        quantize(1, 0, T)
-        gather_codes(1, 0, 512)
-        quantize(2, 0, T)
-        gather_codes(1, 512, SLOTS)
-        gather_codes(2, 0, 512)
-        quantize(3, 0, T)
-        gather_codes(2, 512, SLOTS)
-        gather(slot_packed, scales[:, T : T + WINDOW], 0, SLOTS)
-        for a in range(1, 4):
-            for r in range(4):
-                nc.sync.dma_start(moved[a - 1][r:P:32].bitcast(I32), slot_packed[4 * a + r : P : 32].bitcast(I32))
-        nc.sync.dma_start(pos1_sb[:], pos1)
-        nc.sync.dma_start(pos2_sb[:], pos2)
-        for i in range(2):
-            nc.sync.dma_start(gate_sb[i][:], gate[i])
-        quantize(4, 0, T)
-        for i in range(BLOCKS):
-            multiply(0, i)
-        gather_codes(3, 0, SLOTS)
-        for a in (1, 2, 3):
+        for a in range(SHARED):
             for i in range(BLOCKS):
                 multiply(a, i)
         gather(slot_last, scales[:, 0:WINDOW], 0, SLOTS)
-        for s0, s1 in LAST_CODE_PIECES:
+        for s0, s1 in ((0, 512), (512, 896), (896, 1024)):
             gather_codes(4, s0, s1)
             for i in range(s0 // BLOCK, s1 // BLOCK):
                 multiply(4, i)
@@ -162,11 +163,11 @@ def tile_moe_rag_lin_silu_kernel(tc, xT, w_words, w_scales, b, gate, offs, pos1,
             e = BLOCK_EXPERT[i]
             nc.scalar.activation(y[:, i * BLOCK : (i + 1) * BLOCK], banks[i][:], SILU, bias=b_sb[:, e : e + 1])
 
-        nc.vector.tensor_tensor(part1[:], y[:].indirect(pos1_sb[:]), gate_sb[0][:], MULT)
+        nc.vector.tensor_tensor(part1[:], y[:].indirect(pos1_sb[:]), gate_sb[:, 0, :], MULT)
         parts = (slice(0, 384), slice(384, T))
         for cols in parts:
             listed = pos2_sb[:, cols.start // 16 : cols.stop // 16]
-            nc.vector.tensor_tensor(part2[:, cols], y[:].indirect(listed), gate_sb[1][:, cols], MULT)
+            nc.vector.tensor_tensor(part2[:, cols], y[:].indirect(listed), gate_sb[:, 1, cols], MULT)
         for cols in parts:
             nc.vector.tensor_tensor(result[:, cols], part1[:, cols], part2[:, cols], ADD)
             nc.sync.dma_start(out[:, cols], result[:, cols])

from contextlib import ExitStack

import concourse.mybir as mybir

K, T, N = 2560, 512, 128
COUNTS = (128, 384, 256, 256)
E = len(COUNTS)
SLOTS = sum(COUNTS)

FLOPS = 2 * K * N * SLOTS

F32 = mybir.dt.float32
BF16 = mybir.dt.bfloat16
U32 = mybir.dt.uint32
I32 = mybir.dt.int32
U16 = mybir.dt.uint16
U8 = mybir.dt.uint8
FP8X4 = mybir.dt.float8_e4m3fn_x4
FP4X4 = mybir.dt.float4_e2m1fn_x4
SILU = mybir.ActivationFunctionType.Silu
MULT = mybir.AluOpType.mult
ADD = mybir.AluOpType.add

P = 128
PACK = 4
K_PASS = P * PACK
PASSES = K // K_PASS
SHARED = 4
BLOCK = 128
BLOCKS = SLOTS // BLOCK
BLOCK_EXPERT = [e for e in range(E) for i in range(COUNTS[e] // BLOCK)]
WINDOW = 1536
HALF = T // 2


def tile_moe_rag_lin_silu_kernel(tc, xT, w_words, w_scales, b, gate, offs, pos1, pos2, out):
    nc = tc.nc
    with ExitStack() as ctx:
        keep = ctx.enter_context(tc.tile_pool(name="keep", bufs=1))
        psum = ctx.enter_context(tc.psum_pool(name="psum", bufs=1))

        offs_sb = keep.tile([P, SLOTS // 16], U16)
        pos1_sb = keep.tile([P, T // 16], U16)
        pos2_sb = keep.tile([P, T // 16], U16)
        raw = [keep.tile([P, PACK, T], F32, name=f"raw{a}", tag=f"turn{a}", align_bytes=64) for a in range(PASSES)]
        grouped = [keep.tile([P, T * PACK], BF16, name=f"grouped{a}", align_bytes=64) for a in range(PASSES)]
        codes = keep.tile([P, (PASSES - 1) * T + WINDOW], I32, align_bytes=64)
        scales = keep.tile([P, T + WINDOW], U8, align_bytes=64)
        slot_codes = [keep.tile([P, SLOTS], U32, name=f"slot_codes{a}", align_bytes=64) for a in range(PASSES)]
        slot_shared = keep.tile([P, SLOTS], U8, align_bytes=64)
        slot_last = keep.tile([P, SLOTS], U8, align_bytes=64)
        moved = [keep.tile([P, SLOTS], U8, name=f"moved{a}", align_bytes=64) for a in range(1, SHARED)]
        slot_scales = [slot_shared] + moved + [slot_last]
        ws_sb = keep.tile([P, E * PASSES, N], U8, align_bytes=64)
        b_sb = keep.tile([P, E], F32)
        y = keep.tile([P, SLOTS], F32)
        part1 = keep.tile([P, T], F32)
        part2 = keep.tile([P, T], F32)
        result = keep.tile([P, T], F32)
        warm = keep.tile([P, 8], F32)
        banks = [psum.tile([P, BLOCK], F32, name=f"bank{i}") for i in range(BLOCKS)]

        nc.vector.memset(warm[:, 0:1], 0.0)
        nc.scalar.activation(warm[:, 4:5], warm[:, 0:1], SILU)
        nc.vector.memset(codes[:, PASSES * T :], 0)
        nc.gpsimd.memset(scales[:].bitcast(I32), 0)
        nc.gpsimd.memset(ws_sb[:].rearrange("p i n -> p (i n)").bitcast(I32), 0)
        for plane in moved:
            nc.gpsimd.memset(plane[:].bitcast(I32), 0)

        def x_rows(a):
            return xT[a * K_PASS : (a + 1) * K_PASS, :].rearrange("(p j) t -> p j t", j=PACK)

        for a in range(2):
            for t0 in (0, HALF):
                nc.sync.dma_start(raw[a][:, :, t0 : t0 + HALF], x_rows(a)[:, :, t0 : t0 + HALF])
            if a == 0:
                nc.sync.dma_start(offs_sb[:], offs)
        for a in range(2, PASSES):
            nc.sync.dma_start(raw[a][:], x_rows(a))
        ws_words = w_scales.bitcast(I32).rearrange("e a q n -> q (e a) n")
        for q in range(4):
            nc.sync.dma_start(ws_sb[32 * q : 32 * q + 4].bitcast(I32), ws_words[4 * q : 4 * q + 4])
        nc.sync.dma_start(b_sb[:], b)

        def interleave(copy, a, t0, t1):
            dst = grouped[a][:, PACK * t0 : PACK * t1].rearrange("p (c i j) -> p c j i", i=4, j=PACK)
            copy(dst, raw[a][:, :, t0:t1].rearrange("p j (c i) -> p c j i", i=4))

        def quantize(a, t0, t1):
            place = T * (PASSES - 1 - a)
            nc.vector.quantize_mx(
                out=codes[:, place + t0 : place + t1].bitcast(FP8X4),
                scales=scales[4 * a : P, T + t0 : T + t1] if a < SHARED else scales[:, t0:t1],
                in_=grouped[a][:, PACK * t0 : PACK * t1],
            )

        def gather(dst, window, s0, s1):
            nc.vector.tensor_copy(dst[:, s0:s1], window.indirect(offs_sb[:, s0 // 16 : s1 // 16]))

        def gather_codes(a, s0, s1):
            place = T * (PASSES - 1 - a)
            width = WINDOW if s1 - s0 > 128 else 2 * T
            gather(slot_codes[a], codes[:, place : place + width].bitcast(U32), s0, s1)

        for t0 in (0, HALF):
            interleave(nc.vector.tensor_copy, 0, t0, t0 + 144)
            interleave(nc.scalar.copy, 0, t0 + 144, t0 + HALF)
            quantize(0, t0, t0 + HALF)
        interleave(nc.vector.tensor_copy, 1, 0, 128)
        interleave(nc.scalar.copy, 1, 128, HALF)
        interleave(nc.scalar.copy, 1, HALF, T)
        gather_codes(0, 0, SLOTS)
        interleave(nc.scalar.copy, 2, 128, T)
        quantize(1, 0, T)
        gather_codes(1, 0, 512)
        interleave(nc.vector.tensor_copy, 2, 0, 128)
        interleave(nc.scalar.copy, 3, 224, T)
        gather_codes(1, 512, SLOTS)
        quantize(2, 0, T)
        interleave(nc.vector.tensor_copy, 3, 0, 224)
        w_sb = keep.tile([P, E * PASSES, 2 * N], U8, name="w_sb", tag="turn3", align_bytes=64)
        nc.scalar.dma_start(w_sb[:].bitcast(I32), w_words.bitcast(I32).rearrange("e a p n -> p (e a) n"))
        interleave(nc.scalar.copy, 4, 0, T)
        gather_codes(2, 0, 256)
        quantize(3, 0, T)
        gather_codes(2, 256, 512)
        gather(slot_shared, scales[:, T : T + WINDOW], 0, SLOTS)
        for a in range(1, SHARED):
            for r in range(4):
                nc.sync.dma_start(moved[a - 1][r:P:32].bitcast(I32), slot_shared[4 * a + r : P : 32].bitcast(I32))
        gather_codes(2, 512, SLOTS)
        nc.sync.dma_start(pos1_sb[:], pos1)
        nc.sync.dma_start(pos2_sb[:], pos2)
        gate_sb = keep.tile([P, 2, T], F32, name="gate_sb", tag="turn4", align_bytes=64)
        nc.sync.dma_start(gate_sb[:], gate.rearrange("g p t -> p g t"))
        gather_codes(3, 0, 768)
        quantize(4, 0, T)
        gather_codes(3, 768, SLOTS)

        def multiply(a, i):
            e = BLOCK_EXPERT[i]
            cols = slice(i * BLOCK, (i + 1) * BLOCK)
            nc.tensor.matmul_mx(
                out=banks[i][:],
                lhsT=w_sb[:, e * PASSES + a, :].bitcast(FP4X4),
                lhsT_scale=ws_sb[:, e * PASSES + a, :],
                rhs=slot_codes[a][:, cols].bitcast(FP8X4),
                rhs_scale=slot_scales[a][:, cols],
                start=(a == 0),
                stop=(a == PASSES - 1),
            )

        for a in range(SHARED):
            for i in range(BLOCKS):
                multiply(a, i)
        gather(slot_last, scales[:, 0:WINDOW], 0, SLOTS)
        for s0, s1 in ((0, 512), (512, 896), (896, 1024)):
            gather_codes(4, s0, s1)
            for i in range(s0 // BLOCK, s1 // BLOCK):
                multiply(4, i)
        for i in range(BLOCKS):
            e = BLOCK_EXPERT[i]
            nc.scalar.activation(y[:, i * BLOCK : (i + 1) * BLOCK], banks[i][:], SILU, bias=b_sb[:, e : e + 1])

        nc.vector.tensor_tensor(part1[:], y[:].indirect(pos1_sb[:]), gate_sb[:, 0, :], MULT)
        parts = (slice(0, 384), slice(384, T))
        for cols in parts:
            listed = pos2_sb[:, cols.start // 16 : cols.stop // 16]
            nc.vector.tensor_tensor(part2[:, cols], y[:].indirect(listed), gate_sb[:, 1, cols], MULT)
        for cols in parts:
            nc.vector.tensor_tensor(result[:, cols], part1[:, cols], part2[:, cols], ADD)
            nc.sync.dma_start(out[:, cols], result[:, cols])
